import numpy as np
import ml_dtypes


def mxq(x, axis, fmt="e4m3"):
    dtype, down = {"e4m3": (ml_dtypes.float8_e4m3fn, 7), "e5m2": (ml_dtypes.float8_e5m2, 14)}[fmt]
    v = np.moveaxis(np.asarray(x, np.float32).astype(ml_dtypes.bfloat16).astype(np.float64), axis, -1)
    blocks = v.reshape(v.shape[:-1] + (-1, 32))
    amax = np.abs(blocks).max(-1, keepdims=True)
    byte = np.maximum(np.where(amax > 0, np.frexp(amax)[1] - 1 + 127, 0) - down, 1)
    scale = np.exp2(byte - 127.0)
    codes = (blocks / scale).astype(np.float32).astype(dtype).astype(np.float64)
    return np.moveaxis((codes * scale).reshape(v.shape), -1, axis)


WIDE = False


def mx_kscale(k):
    if not WIDE:
        return np.ones(k)
    levels = np.array([10, -10, 5, -5, 0])
    if k % 512:
        return np.exp2(np.random.permutation(np.resize(levels, k // 32))).repeat(32)
    a = np.empty((k // 512, 16))
    for p in range(k // 512):
        a[p, :8] = np.random.permutation(np.resize(levels, 8))
        for g in range(8):
            far = levels[np.abs(levels - a[p, g]) >= 10]
            a[p, g + 8] = far[np.random.randint(len(far))]
    return np.exp2(a.ravel()).repeat(32)


BF16 = ml_dtypes.bfloat16


def bf(x):
    return np.asarray(x, np.float32).astype(BF16)


def f64(x):
    return np.asarray(x).astype(np.float64)


E2M1 = np.array([0.0, 0.5, 1.0, 1.5, 2.0, 3.0, 4.0, 6.0, -0.0, -0.5, -1.0, -1.5, -2.0, -3.0, -4.0, -6.0])


def pack_weight(w, fmt):
    k, n = w.shape
    w = f64(bf(w)).reshape(k // 32, 32, n)
    amax = np.abs(w).max(1)
    if fmt == "e4m3":
        byte = np.frexp(amax)[1] - 1 + 127 - 7
    else:
        mant, ex = np.frexp(amax / 6.0)
        byte = np.where(mant > 0.5, ex, ex - 1) + 127
    byte = np.clip(np.where(amax > 0, byte, 1), 1, 254)
    scaled = (w * np.exp2(127.0 - byte)[:, None, :]).reshape(k, n).astype(np.float32)
    by_word = np.ascontiguousarray(scaled.reshape(k // 512, 128, 4, n).transpose(0, 1, 3, 2))
    if fmt == "e4m3":
        words = by_word.astype(ml_dtypes.float8_e4m3fn).view(np.uint8)
    else:
        c = by_word.astype(ml_dtypes.float4_e2m1fn).view(np.uint8) & 0xF
        words = c[..., 0::2] | (c[..., 1::2] << 4)
    return np.ascontiguousarray(words), np.ascontiguousarray(byte.astype(np.uint8).reshape(k // 512, 16, n))


def unpack_weight(words, scales, fmt):
    g, p, n, _ = words.shape
    if fmt == "e4m3":
        vals = np.ascontiguousarray(words).view(ml_dtypes.float8_e4m3fn).astype(np.float64)
    else:
        nib = np.empty((g, p, n, 4), np.uint8)
        nib[..., 0::2] = words & 0xF
        nib[..., 1::2] = words >> 4
        vals = E2M1[nib]
    vals = vals * np.repeat(np.exp2(scales.astype(np.float64) - 127.0), 8, axis=1)[..., None]
    return vals.transpose(0, 1, 3, 2).reshape(g * 512, n)
def pack4(w):
    words, scales = pack_weight(w, "e2m1")
    return words.reshape(words.shape[0], 128, -1), scales


def unpack4(words, scales):
    return unpack_weight(words.reshape(words.shape[0], 128, -1, 2), scales, "e2m1")


M, N, D = 2048, 1024, 1024

TEMPERATURE = 2.0
BIAS_MEAN = -1.0


def draw0():
    s = mx_kscale(D)
    t = mx_kscale(M)
    a = np.random.standard_normal((M, D))
    c = TEMPERATURE * np.random.standard_normal((N, D)) / np.sqrt(D)
    bank_words, bank_scales = pack4(a / np.sqrt(M) / t[:, None])
    return {"audio": bf(a * s),
            "captions": bf(c / s),
            "bias": bf(BIAS_MEAN + 0.5 * np.random.standard_normal(N)),
            "clip_weight": bf((1 + 0.1 * np.random.standard_normal(M)) * t),
            "bank_words": bank_words,
            "bank_scales": bank_scales}


def core(audio, captions, bias, clip_weight, bank_words, bank_scales):
    qa = mxq(f64(audio), 1, "e4m3")
    qc = mxq(f64(captions), 1, "e4m3")
    logits = (qa @ qc.T) + f64(bias)
    prob = 1.0 / (1.0 + np.exp(-logits))
    resid = prob * f64(clip_weight)[:, None]
    qr = mxq(resid, 0, "e4m3")
    bank = unpack4(bank_words, bank_scales)
    return qr.T @ bank


def e4m3fn_bytes(y):
    return np.clip(np.asarray(y, np.float64), -448.0, 448.0).astype(np.float32).astype(ml_dtypes.float8_e4m3fn).view(np.uint8)


def e4m3fn_values(b):
    return np.asarray(b, np.uint8).view(ml_dtypes.float8_e4m3fn).astype(np.float64)


def setup_inputs():
    d = draw0()
    x0 = np.asarray(d['audio']).astype(np.float64)
    s = (np.max(np.abs(x0), axis=(0,), keepdims=True) / 448.0).astype(np.float32)
    out = {}
    for k, v in d.items():
        if k == 'audio':
            out['audio_bytes'] = e4m3fn_bytes(x0 / s.astype(np.float64))
            out['audio_scale'] = s
        else:
            out[k] = v
    return out


def reference(audio_bytes, audio_scale, captions, bias, clip_weight, bank_words, bank_scales):
    return core(e4m3fn_values(audio_bytes) * audio_scale.astype(np.float64), captions, bias, clip_weight, bank_words, bank_scales)

@@ -1,0 +1,332 @@
+from contextlib import ExitStack
+
+import concourse.mybir as mybir
+from concourse.masks import make_identity
+
+F32 = mybir.dt.float32
+BF16 = mybir.dt.bfloat16
+U32 = mybir.dt.uint32
+I32 = mybir.dt.int32
+U8 = mybir.dt.uint8
+FP8 = mybir.dt.float8_e4m3fn
+FP8X4 = mybir.dt.float8_e4m3fn_x4
+FP4X4 = mybir.dt.float4_e2m1fn_x4
+MULT = mybir.AluOpType.mult
+SIGMOID = mybir.ActivationFunctionType.Sigmoid
+
+CLIPS, CAPS, FEATS = 2048, 1024, 1024
+P = 128
+CHUNK = 512
+CHUNKS = CLIPS // CHUNK
+PASSES = FEATS // CHUNK
+CAP_TILES = CAPS // P
+EARLY = 4
+
+FLOPS = 2 * 2 * CLIPS * CAPS * FEATS
+
+
+def tile_siglip_negative_caption_gradient_s13_kernel(
+    tc, audio_bytes, audio_scale, captions, bias, clip_weight, bank_words, bank_scales, out
+):
+    nc = tc.nc
+    with ExitStack() as ctx:
+        keep = ctx.enter_context(tc.tile_pool(name="keep", bufs=1))
+        work = ctx.enter_context(tc.tile_pool(name="work", bufs=3))
+        psum = ctx.enter_context(tc.psum_pool(name="psum", bufs=2))
+
+        scale_all = keep.tile([P, FEATS], F32, name="scale_all")
+        raw = [keep.tile([P, 4 * FEATS], U8, name="raw%d" % g) for g in range(CHUNKS)]
+        cap = [keep.tile([P, FEATS], BF16, name="cap%d" % t) for t in range(CAP_TILES)]
+        weight_all = keep.tile([P, CLIPS], BF16, name="weight_all")
+        weight_ord = keep.tile([P, CLIPS], BF16, name="weight_ord")
+        bias_rows = keep.tile([P, P], BF16, name="bias_rows")
+        bias_cols = keep.tile([P, CAP_TILES], F32, name="bias_cols")
+        bank = keep.tile([P, CHUNKS, 2 * FEATS], U8, align_bytes=64, name="bank")
+        bank_sc = keep.tile([P, CHUNKS, FEATS], U8, align_bytes=64, name="bank_sc")
+        ident = keep.tile([P, P], F32, name="ident")
+        ident_b = keep.tile([P, P], BF16, name="ident_b")
+        dummy = keep.tile([P, 1], F32, name="dummy")
+        aud_codes = keep.tile([P, CHUNKS, PASSES, CHUNK], U32, align_bytes=64, name="aud_codes")
+        aud_planes = keep.tile([P, CHUNKS, PASSES, CHUNK], U8, align_bytes=64, name="aud_planes")
+        cap_codes = keep.tile([P, CAP_TILES, PASSES, P], U32, align_bytes=64, name="cap_codes")
+        cap_planes = keep.tile([P, CAP_TILES, PASSES, P], U8, align_bytes=64, name="cap_planes")
+        r_codes = keep.tile([P, 2, 4, 4, P], U32, align_bytes=64, name="r_codes")
+        r_planes = keep.tile([P, 2, 4, 4, P], U8, align_bytes=64, name="r_planes")
+
+        nc.vector.memset(dummy[:], 0.0)
+        nc.vector.memset(bias_rows[:], 0.0)
+        nc.scalar.activation(out=dummy[:], in_=dummy[:], func=SIGMOID)
+        make_identity(nc, ident[:])
+        make_identity(nc, ident_b[:])
+        nc.gpsimd.memset(bank_sc[:].rearrange("p g d -> p (g d)").bitcast(U32), 0)
+
+        aud_view = audio_bytes.rearrange("(g q s) d -> g q (s d)", q=P, s=4)
+        cap_view = captions.rearrange("(t p) d -> t p d", p=P)
+        half = 2 * FEATS
+        nc.sync.dma_start(out=scale_all[:], in_=audio_scale.rearrange("o d -> (o d)").partition_broadcast(P))
+        nc.sync.dma_start(out=raw[0][:, :half], in_=aud_view[0][:, :half])
+        nc.sync.dma_start(out=cap[0][:], in_=cap_view[0])
+        nc.sync.dma_start(out=raw[0][:, half:], in_=aud_view[0][:, half:])
+        nc.sync.dma_start(out=cap[1][:], in_=cap_view[1])
+        nc.sync.dma_start(out=bias_rows[0:CAP_TILES, :], in_=bias.rearrange("(t p) -> t p", p=P))
+        nc.sync.dma_start(out=cap[2][:], in_=cap_view[2])
+        nc.sync.dma_start(out=cap[3][:], in_=cap_view[3])
+        nc.sync.dma_start(out=raw[1][:], in_=aud_view[1])
+        nc.sync.dma_start(out=weight_all[:], in_=clip_weight.partition_broadcast(P))
+        nc.sync.dma_start(out=cap[4][:], in_=cap_view[4])
+        nc.sync.dma_start(out=cap[5][:], in_=cap_view[5])
+        nc.sync.dma_start(out=raw[2][:], in_=aud_view[2])
+        for q in range(4):
+            nc.sync.dma_start(
+                out=bank_sc[32 * q : 32 * q + 4, :, :].bitcast(I32),
+                in_=bank_scales[:, 4 * q : 4 * q + 4, :].rearrange("g r n -> r g n").bitcast(I32),
+            )
+        nc.sync.dma_start(out=bank[:], in_=bank_words.rearrange("g p n -> p g n"))
+        nc.sync.dma_start(out=cap[6][:], in_=cap_view[6])
+        nc.sync.dma_start(out=cap[7][:], in_=cap_view[7])
+        nc.sync.dma_start(out=raw[3][:], in_=aud_view[3])
+
+        def cap_turn(t):
+            xt = psum.tile([P, PASSES, 2, P], F32, tag="turn", name="xt")
+            words = cap[t][:].bitcast(F32)
+            for h in range(PASSES):
+                for u in range(2):
+                    nc.tensor.transpose(xt[:, h, u, :], words[:, 256 * h + u : 256 * (h + 1) : 2], ident[:])
+            grouped = work.tile([P, 1024], BF16, align_bytes=64, tag="cap_grouped", name="cap_grouped")
+            nc.scalar.copy(
+                out=grouped[:].bitcast(F32).rearrange("p (h j u) -> p h j u", h=PASSES, u=2),
+                in_=xt[:].rearrange("p h u j -> p h j u"),
+            )
+            return grouped
+
+        def cap_quant(t, grouped):
+            nc.vector.quantize_mx(
+                out=cap_codes[:, t, :, :].rearrange("p h j -> p (h j)").bitcast(FP8X4),
+                scales=cap_planes[:, t, :, :].rearrange("p h j -> p (h j)"),
+                in_=grouped[:],
+            )
+
+        audio = {}
+
+        def widen(g, s):
+            if s == 0:
+                audio[g] = work.tile([P, 4, FEATS], BF16, align_bytes=64, tag="audio", name="audio")
+            nc.vector.tensor_tensor(
+                out=audio[g][:, s, :],
+                in0=raw[g][:, s * FEATS : (s + 1) * FEATS].bitcast(FP8),
+                in1=scale_all[:],
+                op=MULT,
+            )
+
+        def aud_turn(g, top):
+            res = []
+            for h in range(PASSES):
+                xt = psum.tile([P, 2, 2, P], F32, tag="turn", name="xt")
+                for u in range(2):
+                    for e in range(2):
+                        words = audio[g][:, 2 * top + e, :].bitcast(F32)
+                        nc.tensor.transpose(xt[:, u, e, :], words[:, 256 * h + u : 256 * (h + 1) : 2], ident[:])
+                grouped = work.tile([P, 1024], BF16, align_bytes=64, tag="aud_grouped", name="aud_grouped", bufs=4)
+                nc.scalar.copy(
+                    out=grouped[:].bitcast(F32).rearrange("p (q e u) -> p q e u", e=2, u=2),
+                    in_=xt[:].rearrange("p u e q -> p q e u"),
+                )
+                res.append(grouped)
+            return res
+
+        def aud_quant(g, top, res):
+            for h in range(PASSES):
+                cols = slice(256 * top, 256 * (top + 1))
+                nc.vector.quantize_mx(
+                    out=aud_codes[:, g, h, cols].bitcast(FP8X4), scales=aud_planes[:, g, h, cols], in_=res[h][:]
+                )
+
+        def logits(t, g, sig):
+            acc = psum.tile([P, CHUNK], F32, tag="logit", name="acc")
+            for h in range(PASSES):
+                nc.tensor.matmul_mx(
+                    out=acc[:],
+                    lhsT=cap_codes[:, t, h, :].bitcast(FP8X4),
+                    lhsT_scale=cap_planes[:, t, h, :],
+                    rhs=aud_codes[:, g, h, :].bitcast(FP8X4),
+                    rhs_scale=aud_planes[:, g, h, :],
+                    start=(h == 0),
+                    stop=(h == PASSES - 1),
+                )
+            nc.scalar.activation(out=sig, in_=acc[:], func=SIGMOID, bias=bias_cols[:, t : t + 1])
+
+        def pair_logits(units):
+            sig = work.tile([P, 2, CHUNK], F32, tag="sig", name="sig")
+            for a, (t, g) in enumerate(units):
+                logits(t, g, sig[:, a, :])
+            return sig
+
+        def pair_weigh(units, sig):
+            resid = work.tile([P, 2, CHUNK], BF16, align_bytes=64, tag="resid", name="resid")
+            (t0, g0), (t1, g1) = units
+            if g0 == g1:
+                w = weight_ord[:, g0 * CHUNK : (g0 + 1) * CHUNK].unsqueeze(1).to_broadcast([P, 2, CHUNK])
+            else:
+                w = weight_ord[:, g0 * CHUNK : (g0 + 2) * CHUNK].rearrange("p (a c) -> p a c", a=2)
+            nc.vector.tensor_tensor(out=resid[:], in0=sig[:], in1=w, op=MULT)
+            return resid
+
+        def pair_turn(resid):
+            xt = psum.tile([P, 2, 2, P], F32, tag="turn", name="xt")
+            for a in range(2):
+                words = resid[:, a, :].bitcast(F32)
+                for top in range(2):
+                    nc.tensor.transpose(xt[:, a, top, :], words[:, P * top : P * (top + 1)], ident[:])
+            grouped = work.tile([P, 1024], BF16, align_bytes=64, tag="r_grouped", name="r_grouped")
+            nc.scalar.copy(
+                out=grouped[:].bitcast(F32).rearrange("p (a j u) -> p a j u", a=2, u=2),
+                in_=xt[:].rearrange("p a u j -> p a j u"),
+            )
+            return grouped
+
+        def place(t, g):
+            return (0, g, t) if t < EARLY else (1, t - EARLY, g)
+
+        def pair_quant(units, grouped):
+            sweep, x, y = place(*units[0])
+            nc.vector.quantize_mx(
+                out=r_codes[:, sweep, x, y : y + 2, :].rearrange("p a j -> p (a j)").bitcast(FP8X4),
+                scales=r_planes[:, sweep, x, y : y + 2, :].rearrange("p a j -> p (a j)"),
+                in_=grouped[:],
+            )
+
+        sums = {}
+
+        def grad(t, chunks):
+            for h in range(2):
+                if chunks[0] == 0:
+                    sums[t, h] = psum.tile([P, 512], F32, tag="grad", name="gradsum", bufs=4)
+                for g in chunks:
+                    sweep, x, y = place(t, g)
+                    nc.tensor.matmul_mx(
+                        out=sums[t, h][:],
+                        lhsT=r_codes[:, sweep, x, y, :].bitcast(FP8X4),
+                        lhsT_scale=r_planes[:, sweep, x, y, :],
+                        rhs=bank[:, g, 1024 * h : 1024 * (h + 1)].bitcast(FP4X4),
+                        rhs_scale=bank_sc[:, g, 512 * h : 512 * (h + 1)],
+                        start=(g == 0),
+                        stop=(g == CHUNKS - 1),
+                    )
+
+        def finish(t):
+            res = work.tile([P, FEATS], F32, tag="res", name="res")
+            last = t == CAP_TILES - 1
+            for h in range(2):
+                cols = slice(512 * h, 512 * (h + 1))
+                if last and h == 0:
+                    nc.scalar.copy(out=res[:, cols], in_=sums[t, h][:])
+                else:
+                    nc.vector.tensor_copy(out=res[:, cols], in_=sums[t, h][:])
+                if last:
+                    nc.sync.dma_start(out=out[t * P : (t + 1) * P, cols], in_=res[:, cols])
+            if not last:
+                nc.sync.dma_start(out=out[t * P : (t + 1) * P, :], in_=res[:])
+
+        ctx.enter_context(tc.manual_schedule())
+        widen(0, 0)
+        c0 = cap_turn(0)
+        widen(0, 1)
+        cap_quant(0, c0)
+        c1 = cap_turn(1)
+        a0 = aud_turn(0, 0)
+        widen(0, 2)
+        cap_quant(1, c1)
+        widen(0, 3)
+        c2 = cap_turn(2)
+        aud_quant(0, 0, a0)
+        bias_ps = psum.tile([P, P], BF16, tag="turn", name="bias_ps")
+        nc.tensor.transpose(bias_ps[:], bias_rows[:], ident_b[:])
+        nc.vector.tensor_copy(out=bias_cols[:], in_=bias_ps[:, 0:CAP_TILES])
+        a1 = aud_turn(0, 1)
+        c3 = cap_turn(3)
+        widen(1, 0)
+        cap_quant(2, c2)
+        aud_quant(0, 1, a1)
+        cap_quant(3, c3)
+        nc.scalar.copy(
+            out=weight_ord[:].rearrange("p (g u q e) -> p g u q e", g=CHUNKS, u=2, e=2)[:, 0],
+            in_=weight_all[:].rearrange("p (g q u e) -> p g u q e", g=CHUNKS, u=2, e=2)[:, 0],
+        )
+        widen(1, 1)
+        nxt = aud_turn(1, 0)
+
+        for g in range(CHUNKS):
+            more = g + 1 < CHUNKS
+            p0 = [(0, g), (1, g)]
+            p1 = [(2, g), (3, g)]
+            s0 = pair_logits(p0)
+            s1 = pair_logits(p1)
+            if g > 0:
+                grad(0, [g - 1])
+                grad(1, [g - 1])
+            if g == 0:
+                for k in range(1, CHUNKS):
+                    nc.scalar.copy(
+                        out=weight_ord[:].rearrange("p (g u q e) -> p g u q e", g=CHUNKS, u=2, e=2)[:, k],
+                        in_=weight_all[:].rearrange("p (g q u e) -> p g u q e", g=CHUNKS, u=2, e=2)[:, k],
+                    )
+            if more:
+                widen(g + 1, 2)
+            w0 = pair_weigh(p0, s0)
+            if more:
+                widen(g + 1, 3)
+                aud_quant(g + 1, 0, nxt)
+            r0 = pair_turn(w0)
+            if more:
+                b1 = aud_turn(g + 1, 1)
+            w1 = pair_weigh(p1, s1)
+            pair_quant(p0, r0)
+            r1 = pair_turn(w1)
+            if g + 2 < CHUNKS:
+                widen(g + 2, 0)
+            late = (4, 5) if g == 1 else (6, 7) if g == 2 else ()
+            gl = [cap_turn(t) for t in late]
+            pair_quant(p1, r1)
+            if g + 2 < CHUNKS:
+                widen(g + 2, 1)
+                nxt = aud_turn(g + 2, 0)
+            for t, x in zip(late, gl):
+                cap_quant(t, x)
+            if more:
+                aud_quant(g + 1, 1, b1)
+
+        def first(t):
+            units = [[(t, 0), (t, 1)], [(t, 2), (t, 3)]]
+            return units, [pair_logits(x) for x in units]
+
+        def middle(units, sigs):
+            ws = [pair_weigh(x, s) for x, s in zip(units, sigs)]
+            gs = [pair_turn(w) for w in ws]
+            for x, r in zip(units, gs):
+                pair_quant(x, r)
+
+        every = list(range(CHUNKS))
+        f4 = first(4)
+        grad(0, [3])
+        grad(1, [3])
+        finish(0)
+        finish(1)
+        grad(2, every)
+        f5 = first(5)
+        middle(*f4)
+        finish(2)
+        grad(3, every)
+        f6 = first(6)
+        middle(*f5)
+        finish(3)
+        grad(4, every)
+        f7 = first(7)
+        middle(*f6)
+        finish(4)
+        grad(5, every)
+        middle(*f7)
+        finish(5)
+        grad(6, every)
+        finish(6)
+        grad(7, every)
+        finish(7)

@@ -20,7 +20,6 @@ CHUNK = 512
 CHUNKS = CLIPS // CHUNK
 PASSES = FEATS // CHUNK
 CAP_TILES = CAPS // P
-EARLY = 4
 
 FLOPS = 2 * 2 * CLIPS * CAPS * FEATS
 
@@ -50,8 +49,8 @@ def tile_siglip_negative_caption_gradient_s13_kernel(
         aud_planes = keep.tile([P, CHUNKS, PASSES, CHUNK], U8, align_bytes=64, name="aud_planes")
         cap_codes = keep.tile([P, CAP_TILES, PASSES, P], U32, align_bytes=64, name="cap_codes")
         cap_planes = keep.tile([P, CAP_TILES, PASSES, P], U8, align_bytes=64, name="cap_planes")
-        r_codes = keep.tile([P, 2, 4, 4, P], U32, align_bytes=64, name="r_codes")
-        r_planes = keep.tile([P, 2, 4, 4, P], U8, align_bytes=64, name="r_planes")
+        r_codes = keep.tile([P, CAP_TILES, CHUNKS, P], U32, align_bytes=64, name="r_codes")
+        r_planes = keep.tile([P, CAP_TILES, CHUNKS, P], U8, align_bytes=64, name="r_planes")
 
         nc.vector.memset(dummy[:], 0.0)
         nc.vector.memset(bias_rows[:], 0.0)
@@ -63,36 +62,39 @@ def tile_siglip_negative_caption_gradient_s13_kernel(
         aud_view = audio_bytes.rearrange("(g q s) d -> g q (s d)", q=P, s=4)
         cap_view = captions.rearrange("(t p) d -> t p d", p=P)
         half = 2 * FEATS
+        def load_cap(t):
+            nc.sync.dma_start(out=cap[t][:], in_=cap_view[t])
+
         nc.sync.dma_start(out=scale_all[:], in_=audio_scale.rearrange("o d -> (o d)").partition_broadcast(P))
         nc.sync.dma_start(out=raw[0][:, :half], in_=aud_view[0][:, :half])
-        nc.sync.dma_start(out=cap[0][:], in_=cap_view[0])
+        load_cap(0)
+        load_cap(1)
         nc.sync.dma_start(out=raw[0][:, half:], in_=aud_view[0][:, half:])
-        nc.sync.dma_start(out=cap[1][:], in_=cap_view[1])
         nc.sync.dma_start(out=bias_rows[0:CAP_TILES, :], in_=bias.rearrange("(t p) -> t p", p=P))
-        nc.sync.dma_start(out=cap[2][:], in_=cap_view[2])
-        nc.sync.dma_start(out=cap[3][:], in_=cap_view[3])
+        load_cap(2)
+        load_cap(3)
         nc.sync.dma_start(out=raw[1][:], in_=aud_view[1])
-        nc.sync.dma_start(out=weight_all[:], in_=clip_weight.partition_broadcast(P))
-        nc.sync.dma_start(out=cap[4][:], in_=cap_view[4])
-        nc.sync.dma_start(out=cap[5][:], in_=cap_view[5])
+        load_cap(4)
+        load_cap(5)
+        load_cap(6)
+        load_cap(7)
         nc.sync.dma_start(out=raw[2][:], in_=aud_view[2])
+        nc.sync.dma_start(out=weight_all[:], in_=clip_weight.partition_broadcast(P))
+        nc.sync.dma_start(out=raw[3][:], in_=aud_view[3])
         for q in range(4):
             nc.sync.dma_start(
                 out=bank_sc[32 * q : 32 * q + 4, :, :].bitcast(I32),
                 in_=bank_scales[:, 4 * q : 4 * q + 4, :].rearrange("g r n -> r g n").bitcast(I32),
             )
         nc.sync.dma_start(out=bank[:], in_=bank_words.rearrange("g p n -> p g n"))
-        nc.sync.dma_start(out=cap[6][:], in_=cap_view[6])
-        nc.sync.dma_start(out=cap[7][:], in_=cap_view[7])
-        nc.sync.dma_start(out=raw[3][:], in_=aud_view[3])
 
         def cap_turn(t):
-            xt = psum.tile([P, PASSES, 2, P], F32, tag="turn", name="xt")
+            xt = psum.tile([P, PASSES, 2, P], F32, tag="turn", name="xt", bufs=4)
             words = cap[t][:].bitcast(F32)
             for h in range(PASSES):
                 for u in range(2):
                     nc.tensor.transpose(xt[:, h, u, :], words[:, 256 * h + u : 256 * (h + 1) : 2], ident[:])
-            grouped = work.tile([P, 1024], BF16, align_bytes=64, tag="cap_grouped", name="cap_grouped")
+            grouped = work.tile([P, 1024], BF16, align_bytes=64, tag="grouped", name="cap_grouped", bufs=7)
             nc.scalar.copy(
                 out=grouped[:].bitcast(F32).rearrange("p (h j u) -> p h j u", h=PASSES, u=2),
                 in_=xt[:].rearrange("p h u j -> p h j u"),
@@ -110,7 +112,7 @@ def tile_siglip_negative_caption_gradient_s13_kernel(
 
         def widen(g, s):
             if s == 0:
-                audio[g] = work.tile([P, 4, FEATS], BF16, align_bytes=64, tag="audio", name="audio")
+                audio[g] = work.tile([P, 4, FEATS], BF16, align_bytes=64, tag="audio", name="audio", bufs=2)
             nc.vector.tensor_tensor(
                 out=audio[g][:, s, :],
                 in0=raw[g][:, s * FEATS : (s + 1) * FEATS].bitcast(FP8),
@@ -121,12 +123,12 @@ def tile_siglip_negative_caption_gradient_s13_kernel(
         def aud_turn(g, top):
             res = []
             for h in range(PASSES):
-                xt = psum.tile([P, 2, 2, P], F32, tag="turn", name="xt")
+                xt = psum.tile([P, 2, 2, P], F32, tag="turn", name="xt", bufs=4)
                 for u in range(2):
                     for e in range(2):
                         words = audio[g][:, 2 * top + e, :].bitcast(F32)
                         nc.tensor.transpose(xt[:, u, e, :], words[:, 256 * h + u : 256 * (h + 1) : 2], ident[:])
-                grouped = work.tile([P, 1024], BF16, align_bytes=64, tag="aud_grouped", name="aud_grouped", bufs=4)
+                grouped = work.tile([P, 1024], BF16, align_bytes=64, tag="grouped", name="aud_grouped", bufs=7)
                 nc.scalar.copy(
                     out=grouped[:].bitcast(F32).rearrange("p (q e u) -> p q e u", e=2, u=2),
                     in_=xt[:].rearrange("p u e q -> p q e u"),
@@ -141,8 +143,14 @@ def tile_siglip_negative_caption_gradient_s13_kernel(
                     out=aud_codes[:, g, h, cols].bitcast(FP8X4), scales=aud_planes[:, g, h, cols], in_=res[h][:]
                 )
 
-        def logits(t, g, sig):
-            acc = psum.tile([P, CHUNK], F32, tag="logit", name="acc")
+        sigs = {}
+        resids = {}
+
+        def logits(t, g):
+            pair = g // 2
+            if g % 2 == 0:
+                sigs[t, pair] = work.tile([P, 2, CHUNK], F32, tag="sig", name="sig", bufs=16)
+            acc = psum.tile([P, CHUNK], F32, tag="sum", name="acc", bufs=4)
             for h in range(PASSES):
                 nc.tensor.matmul_mx(
                     out=acc[:],
@@ -153,60 +161,48 @@ def tile_siglip_negative_caption_gradient_s13_kernel(
                     start=(h == 0),
                     stop=(h == PASSES - 1),
                 )
-            nc.scalar.activation(out=sig, in_=acc[:], func=SIGMOID, bias=bias_cols[:, t : t + 1])
+            nc.scalar.activation(out=sigs[t, pair][:, g % 2, :], in_=acc[:], func=SIGMOID, bias=bias_cols[:, t : t + 1])
 
-        def pair_logits(units):
-            sig = work.tile([P, 2, CHUNK], F32, tag="sig", name="sig")
-            for a, (t, g) in enumerate(units):
-                logits(t, g, sig[:, a, :])
-            return sig
+        def weigh(t, pair):
+            resids[t, pair] = work.tile([P, 2, CHUNK], BF16, align_bytes=64, tag="resid", name="resid", bufs=12)
+            nc.vector.tensor_tensor(
+                out=resids[t, pair][:],
+                in0=sigs[t, pair][:],
+                in1=weight_ord[:, 2 * CHUNK * pair : 2 * CHUNK * (pair + 1)].rearrange("p (a c) -> p a c", a=2),
+                op=MULT,
+            )
 
-        def pair_weigh(units, sig):
-            resid = work.tile([P, 2, CHUNK], BF16, align_bytes=64, tag="resid", name="resid")
-            (t0, g0), (t1, g1) = units
-            if g0 == g1:
-                w = weight_ord[:, g0 * CHUNK : (g0 + 1) * CHUNK].unsqueeze(1).to_broadcast([P, 2, CHUNK])
-            else:
-                w = weight_ord[:, g0 * CHUNK : (g0 + 2) * CHUNK].rearrange("p (a c) -> p a c", a=2)
-            nc.vector.tensor_tensor(out=resid[:], in0=sig[:], in1=w, op=MULT)
-            return resid
-
-        def pair_turn(resid):
-            xt = psum.tile([P, 2, 2, P], F32, tag="turn", name="xt")
+        def pair_turn(t, pair):
+            xt = psum.tile([P, 2, 2, P], F32, tag="turn", name="xt", bufs=4)
             for a in range(2):
-                words = resid[:, a, :].bitcast(F32)
+                words = resids[t, pair][:, a, :].bitcast(F32)
                 for top in range(2):
                     nc.tensor.transpose(xt[:, a, top, :], words[:, P * top : P * (top + 1)], ident[:])
-            grouped = work.tile([P, 1024], BF16, align_bytes=64, tag="r_grouped", name="r_grouped")
+            grouped = work.tile([P, 1024], BF16, align_bytes=64, tag="grouped", name="r_grouped", bufs=7)
             nc.scalar.copy(
                 out=grouped[:].bitcast(F32).rearrange("p (a j u) -> p a j u", a=2, u=2),
                 in_=xt[:].rearrange("p a u j -> p a j u"),
             )
             return grouped
 
-        def place(t, g):
-            return (0, g, t) if t < EARLY else (1, t - EARLY, g)
-
-        def pair_quant(units, grouped):
-            sweep, x, y = place(*units[0])
+        def pair_quant(t, pair, grouped):
+            two = slice(2 * pair, 2 * pair + 2)
             nc.vector.quantize_mx(
-                out=r_codes[:, sweep, x, y : y + 2, :].rearrange("p a j -> p (a j)").bitcast(FP8X4),
-                scales=r_planes[:, sweep, x, y : y + 2, :].rearrange("p a j -> p (a j)"),
+                out=r_codes[:, t, two, :].rearrange("p a j -> p (a j)").bitcast(FP8X4),
+                scales=r_planes[:, t, two, :].rearrange("p a j -> p (a j)"),
                 in_=grouped[:],
             )
 
         sums = {}
 
-        def grad(t, chunks):
+        def grad(t):
             for h in range(2):
-                if chunks[0] == 0:
-                    sums[t, h] = psum.tile([P, 512], F32, tag="grad", name="gradsum", bufs=4)
-                for g in chunks:
-                    sweep, x, y = place(t, g)
+                sums[t, h] = psum.tile([P, 512], F32, tag="sum", name="gradsum", bufs=4)
+                for g in range(CHUNKS):
                     nc.tensor.matmul_mx(
                         out=sums[t, h][:],
-                        lhsT=r_codes[:, sweep, x, y, :].bitcast(FP8X4),
-                        lhsT_scale=r_planes[:, sweep, x, y, :],
+                        lhsT=r_codes[:, t, g, :].bitcast(FP8X4),
+                        lhsT_scale=r_planes[:, t, g, :],
                         rhs=bank[:, g, 1024 * h : 1024 * (h + 1)].bitcast(FP4X4),
                         rhs_scale=bank_sc[:, g, 512 * h : 512 * (h + 1)],
                         start=(g == 0),
@@ -218,14 +214,21 @@ def tile_siglip_negative_caption_gradient_s13_kernel(
             last = t == CAP_TILES - 1
             for h in range(2):
                 cols = slice(512 * h, 512 * (h + 1))
-                if last and h == 0:
-                    nc.scalar.copy(out=res[:, cols], in_=sums[t, h][:])
-                else:
+                if last and h == 1:
                     nc.vector.tensor_copy(out=res[:, cols], in_=sums[t, h][:])
+                else:
+                    nc.scalar.copy(out=res[:, cols], in_=sums[t, h][:])
                 if last:
                     nc.sync.dma_start(out=out[t * P : (t + 1) * P, cols], in_=res[:, cols])
             if not last:
                 nc.sync.dma_start(out=out[t * P : (t + 1) * P, :], in_=res[:])
+
+        def order_weights():
+            for k in range(CHUNKS):
+                nc.scalar.copy(
+                    out=weight_ord[:].rearrange("p (g u q e) -> p g u q e", g=CHUNKS, u=2, e=2)[:, k],
+                    in_=weight_all[:].rearrange("p (g q u e) -> p g u q e", g=CHUNKS, u=2, e=2)[:, k],
+                )
 
         ctx.enter_context(tc.manual_schedule())
         widen(0, 0)
@@ -237,96 +240,91 @@ def tile_siglip_negative_caption_gradient_s13_kernel(
         widen(0, 2)
         cap_quant(1, c1)
         widen(0, 3)
-        c2 = cap_turn(2)
         aud_quant(0, 0, a0)
-        bias_ps = psum.tile([P, P], BF16, tag="turn", name="bias_ps")
+        bias_ps = psum.tile([P, P], BF16, tag="turn", name="bias_ps", bufs=4)
         nc.tensor.transpose(bias_ps[:], bias_rows[:], ident_b[:])
         nc.vector.tensor_copy(out=bias_cols[:], in_=bias_ps[:, 0:CAP_TILES])
         a1 = aud_turn(0, 1)
-        c3 = cap_turn(3)
+        c2 = cap_turn(2)
         widen(1, 0)
         cap_quant(2, c2)
         aud_quant(0, 1, a1)
-        cap_quant(3, c3)
-        nc.scalar.copy(
-            out=weight_ord[:].rearrange("p (g u q e) -> p g u q e", g=CHUNKS, u=2, e=2)[:, 0],
-            in_=weight_all[:].rearrange("p (g q u e) -> p g u q e", g=CHUNKS, u=2, e=2)[:, 0],
-        )
+        c3 = cap_turn(3)
+        c4 = cap_turn(4)
         widen(1, 1)
-        nxt = aud_turn(1, 0)
+        cap_quant(3, c3)
+        cap_quant(4, c4)
+        widen(1, 2)
 
-        for g in range(CHUNKS):
-            more = g + 1 < CHUNKS
-            p0 = [(0, g), (1, g)]
-            p1 = [(2, g), (3, g)]
-            s0 = pair_logits(p0)
-            s1 = pair_logits(p1)
-            if g > 0:
-                grad(0, [g - 1])
-                grad(1, [g - 1])
-            if g == 0:
-                for k in range(1, CHUNKS):
-                    nc.scalar.copy(
-                        out=weight_ord[:].rearrange("p (g u q e) -> p g u q e", g=CHUNKS, u=2, e=2)[:, k],
-                        in_=weight_all[:].rearrange("p (g q u e) -> p g u q e", g=CHUNKS, u=2, e=2)[:, k],
-                    )
-            if more:
-                widen(g + 1, 2)
-            w0 = pair_weigh(p0, s0)
-            if more:
-                widen(g + 1, 3)
-                aud_quant(g + 1, 0, nxt)
-            r0 = pair_turn(w0)
-            if more:
-                b1 = aud_turn(g + 1, 1)
-            w1 = pair_weigh(p1, s1)
-            pair_quant(p0, r0)
-            r1 = pair_turn(w1)
-            if g + 2 < CHUNKS:
-                widen(g + 2, 0)
-            late = (4, 5) if g == 1 else (6, 7) if g == 2 else ()
-            gl = [cap_turn(t) for t in late]
-            pair_quant(p1, r1)
-            if g + 2 < CHUNKS:
-                widen(g + 2, 1)
-                nxt = aud_turn(g + 2, 0)
-            for t, x in zip(late, gl):
-                cap_quant(t, x)
-            if more:
-                aud_quant(g + 1, 1, b1)
+        for t in range(4):
+            logits(t, 0)
+        n0 = aud_turn(1, 0)
+        c5 = cap_turn(5)
+        c6 = cap_turn(6)
+        widen(1, 3)
+        cap_quant(5, c5)
+        aud_quant(1, 0, n0)
+        widen(2, 0)
+        cap_quant(6, c6)
+        n1 = aud_turn(1, 1)
+        c7 = cap_turn(7)
+        for t in range(4, 7):
+            logits(t, 0)
+        widen(2, 1)
+        cap_quant(7, c7)
+        aud_quant(1, 1, n1)
+        logits(7, 0)
+        order_weights()
+        widen(2, 2)
+        widen(2, 3)
+        for g in range(1, CHUNKS):
+            for t in range(4):
+                logits(t, g)
+            if g + 1 < CHUNKS:
+                n0 = aud_turn(g + 1, 0)
+                n1 = aud_turn(g + 1, 1)
+            if g == 1:
+                widen(3, 0)
+                widen(3, 1)
+            if g + 1 < CHUNKS:
+                aud_quant(g + 1, 0, n0)
+            for t in range(4, 8):
+                logits(t, g)
+            if g == 1:
+                widen(3, 2)
+                aud_quant(2, 1, n1)
+                widen(3, 3)
+                for t in range(4):
+                    weigh(t, 0)
+            if g == 2:
+                aud_quant(3, 1, n1)
+                for t in range(4, 8):
+                    weigh(t, 0)
+            if g == 3:
+                for t in range(4):
+                    weigh(t, 1)
 
-        def first(t):
-            units = [[(t, 0), (t, 1)], [(t, 2), (t, 3)]]
-            return units, [pair_logits(x) for x in units]
+        def turns(t):
+            return [pair_turn(t, 0), pair_turn(t, 1)]
 
-        def middle(units, sigs):
-            ws = [pair_weigh(x, s) for x, s in zip(units, sigs)]
-            gs = [pair_turn(w) for w in ws]
-            for x, r in zip(units, gs):
-                pair_quant(x, r)
+        def quants(t, r):
+            pair_quant(t, 0, r[0])
+            pair_quant(t, 1, r[1])
 
-        every = list(range(CHUNKS))
-        f4 = first(4)
-        grad(0, [3])
-        grad(1, [3])
-        finish(0)
-        finish(1)
-        grad(2, every)
-        f5 = first(5)
-        middle(*f4)
-        finish(2)
-        grad(3, every)
-        f6 = first(6)
-        middle(*f5)
-        finish(3)
-        grad(4, every)
-        f7 = first(7)
-        middle(*f6)
-        finish(4)
-        grad(5, every)
-        middle(*f7)
-        finish(5)
-        grad(6, every)
-        finish(6)
-        grad(7, every)
-        finish(7)
+        r0, r1 = turns(0), turns(1)
+        quants(0, r0)
+        quants(1, r1)
+        for t in range(0, CAP_TILES, 2):
+            if t + 4 < CAP_TILES:
+                weigh(t + 4, 1)
+                weigh(t + 5, 1)
+            if t + 2 < CAP_TILES:
+                r0, r1 = turns(t + 2), turns(t + 3)
+            grad(t)
+            if t + 2 < CAP_TILES:
+                quants(t + 2, r0)
+            grad(t + 1)
+            if t + 2 < CAP_TILES:
+                quants(t + 3, r1)
+            finish(t)
+            finish(t + 1)

@@ -71,6 +71,7 @@ def tile_siglip_negative_caption_gradient_s13_kernel(
         load_cap(1)
         nc.sync.dma_start(out=raw[0][:, half:], in_=aud_view[0][:, half:])
         nc.sync.dma_start(out=bias_rows[0:CAP_TILES, :], in_=bias.rearrange("(t p) -> t p", p=P))
+        nc.sync.dma_start(out=weight_all[:], in_=clip_weight.partition_broadcast(P))
         load_cap(2)
         load_cap(3)
         nc.sync.dma_start(out=raw[1][:], in_=aud_view[1])
@@ -79,7 +80,6 @@ def tile_siglip_negative_caption_gradient_s13_kernel(
         load_cap(6)
         load_cap(7)
         nc.sync.dma_start(out=raw[2][:], in_=aud_view[2])
-        nc.sync.dma_start(out=weight_all[:], in_=clip_weight.partition_broadcast(P))
         nc.sync.dma_start(out=raw[3][:], in_=aud_view[3])
         for q in range(4):
             nc.sync.dma_start(
@@ -234,75 +234,27 @@ def tile_siglip_negative_caption_gradient_s13_kernel(
         widen(0, 0)
         c0 = cap_turn(0)
         widen(0, 1)
-        cap_quant(0, c0)
         c1 = cap_turn(1)
         a0 = aud_turn(0, 0)
         widen(0, 2)
-        cap_quant(1, c1)
         widen(0, 3)
+        order_weights()
         aud_quant(0, 0, a0)
         bias_ps = psum.tile([P, P], BF16, tag="turn", name="bias_ps", bufs=4)
         nc.tensor.transpose(bias_ps[:], bias_rows[:], ident_b[:])
+        cap_quant(0, c0)
+        cap_quant(1, c1)
         nc.vector.tensor_copy(out=bias_cols[:], in_=bias_ps[:, 0:CAP_TILES])
         a1 = aud_turn(0, 1)
         c2 = cap_turn(2)
-        widen(1, 0)
-        cap_quant(2, c2)
         aud_quant(0, 1, a1)
         c3 = cap_turn(3)
-        c4 = cap_turn(4)
-        widen(1, 1)
+        cap_quant(2, c2)
+        widen(1, 0)
         cap_quant(3, c3)
-        cap_quant(4, c4)
-        widen(1, 2)
-
-        for t in range(4):
-            logits(t, 0)
-        n0 = aud_turn(1, 0)
+        widen(1, 1)
+        c4 = cap_turn(4)
         c5 = cap_turn(5)
-        c6 = cap_turn(6)
-        widen(1, 3)
-        cap_quant(5, c5)
-        aud_quant(1, 0, n0)
-        widen(2, 0)
-        cap_quant(6, c6)
-        n1 = aud_turn(1, 1)
-        c7 = cap_turn(7)
-        for t in range(4, 7):
-            logits(t, 0)
-        widen(2, 1)
-        cap_quant(7, c7)
-        aud_quant(1, 1, n1)
-        logits(7, 0)
-        order_weights()
-        widen(2, 2)
-        widen(2, 3)
-        for g in range(1, CHUNKS):
-            for t in range(4):
-                logits(t, g)
-            if g + 1 < CHUNKS:
-                n0 = aud_turn(g + 1, 0)
-                n1 = aud_turn(g + 1, 1)
-            if g == 1:
-                widen(3, 0)
-                widen(3, 1)
-            if g + 1 < CHUNKS:
-                aud_quant(g + 1, 0, n0)
-            for t in range(4, 8):
-                logits(t, g)
-            if g == 1:
-                widen(3, 2)
-                aud_quant(2, 1, n1)
-                widen(3, 3)
-                for t in range(4):
-                    weigh(t, 0)
-            if g == 2:
-                aud_quant(3, 1, n1)
-                for t in range(4, 8):
-                    weigh(t, 0)
-            if g == 3:
-                for t in range(4):
-                    weigh(t, 1)
 
         def turns(t):
             return [pair_turn(t, 0), pair_turn(t, 1)]
@@ -311,20 +263,94 @@ def tile_siglip_negative_caption_gradient_s13_kernel(
             pair_quant(t, 0, r[0])
             pair_quant(t, 1, r[1])
 
-        r0, r1 = turns(0), turns(1)
+        for t in range(4):
+            logits(t, 0)
+        cap_quant(4, c4)
+        cap_quant(5, c5)
+        widen(1, 2)
+        n0 = aud_turn(1, 0)
+        c6 = cap_turn(6)
+        c7 = cap_turn(7)
+        widen(1, 3)
+        aud_quant(1, 0, n0)
+        cap_quant(6, c6)
+        cap_quant(7, c7)
+        widen(2, 0)
+        n1 = aud_turn(1, 1)
+        for t in range(4, 8):
+            logits(t, 0)
+        aud_quant(1, 1, n1)
+        widen(2, 1)
+        widen(2, 2)
+        widen(2, 3)
+        for g in range(1, CHUNKS):
+            more = g + 1 < CHUNKS
+            for t in range(4):
+                logits(t, g)
+            if more:
+                n0 = aud_turn(g + 1, 0)
+                n1 = aud_turn(g + 1, 1)
+            if g == 1:
+                widen(3, 0)
+                widen(3, 1)
+            if more:
+                aud_quant(g + 1, 0, n0)
+            if g == 1:
+                widen(3, 2)
+            if more:
+                aud_quant(g + 1, 1, n1)
+                for t in range(4, 8):
+                    logits(t, g)
+            if g == 1:
+                widen(3, 3)
+                for t in range(4):
+                    weigh(t, 0)
+        weigh(0, 1)
+        logits(4, 3)
+        weigh(1, 1)
+        logits(5, 3)
+        weigh(2, 1)
+        r0 = turns(0)
+        r1 = turns(1)
         quants(0, r0)
+        logits(6, 3)
+        logits(7, 3)
+        weigh(3, 1)
         quants(1, r1)
-        for t in range(0, CAP_TILES, 2):
-            if t + 4 < CAP_TILES:
-                weigh(t + 4, 1)
-                weigh(t + 5, 1)
-            if t + 2 < CAP_TILES:
-                r0, r1 = turns(t + 2), turns(t + 3)
-            grad(t)
-            if t + 2 < CAP_TILES:
-                quants(t + 2, r0)
-            grad(t + 1)
-            if t + 2 < CAP_TILES:
-                quants(t + 3, r1)
-            finish(t)
-            finish(t + 1)
+
+        grad(0)
+        finish(0)
+        r2 = turns(2)
+        r3 = turns(3)
+        weigh(4, 0)
+        quants(2, r2)
+        weigh(4, 1)
+        quants(3, r3)
+        grad(1)
+        finish(1)
+        weigh(5, 0)
+        weigh(5, 1)
+        grad(2)
+        finish(2)
+        r4 = turns(4)
+        r5 = turns(5)
+        quants(4, r4)
+        weigh(6, 0)
+        weigh(6, 1)
+        quants(5, r5)
+        grad(3)
+        finish(3)
+        grad(4)
+        finish(4)
+        weigh(7, 0)
+        weigh(7, 1)
+        r6 = turns(6)
+        r7 = turns(7)
+        quants(6, r6)
+        quants(7, r7)
+        grad(5)
+        finish(5)
+        grad(6)
+        finish(6)
+        grad(7)
+        finish(7)

@@ -21,6 +21,8 @@ CHUNKS = CLIPS // CHUNK
 PASSES = FEATS // CHUNK
 CAP_TILES = CAPS // P
 
+SORT = 3
+
 FLOPS = 2 * 2 * CLIPS * CAPS * FEATS
 
 
@@ -36,6 +38,7 @@ def tile_siglip_negative_caption_gradient_s13_kernel(
         scale_all = keep.tile([P, FEATS], F32, name="scale_all")
         raw = [keep.tile([P, 4 * FEATS], U8, name="raw%d" % g) for g in range(CHUNKS)]
         cap = [keep.tile([P, FEATS], BF16, name="cap%d" % t) for t in range(CAP_TILES)]
+        scale_cols = keep.tile([P, 8], F32, name="scale_cols")
         weight_all = keep.tile([P, CLIPS], BF16, name="weight_all")
         weight_ord = keep.tile([P, CLIPS], BF16, name="weight_ord")
         bias_rows = keep.tile([P, P], BF16, name="bias_rows")
@@ -65,28 +68,38 @@ def tile_siglip_negative_caption_gradient_s13_kernel(
         def load_cap(t):
             nc.sync.dma_start(out=cap[t][:], in_=cap_view[t])
 
-        nc.sync.dma_start(out=scale_all[:], in_=audio_scale.rearrange("o d -> (o d)").partition_broadcast(P))
+        nc.sync.dma_start(out=scale_cols[:], in_=audio_scale.rearrange("o (n m) -> (o n) m", m=8))
         nc.sync.dma_start(out=raw[0][:, :half], in_=aud_view[0][:, :half])
         load_cap(0)
-        load_cap(1)
         nc.sync.dma_start(out=raw[0][:, half:], in_=aud_view[0][:, half:])
         nc.sync.dma_start(out=bias_rows[0:CAP_TILES, :], in_=bias.rearrange("(t p) -> t p", p=P))
-        nc.sync.dma_start(out=weight_all[:], in_=clip_weight.partition_broadcast(P))
+        load_cap(1)
         load_cap(2)
         load_cap(3)
         nc.sync.dma_start(out=raw[1][:], in_=aud_view[1])
-        load_cap(4)
-        load_cap(5)
-        load_cap(6)
-        load_cap(7)
+        for t in range(4, CAP_TILES):
+            load_cap(t)
         nc.sync.dma_start(out=raw[2][:], in_=aud_view[2])
         nc.sync.dma_start(out=raw[3][:], in_=aud_view[3])
+        nc.sync.dma_start(out=weight_all[:], in_=clip_weight.partition_broadcast(P))
         for q in range(4):
             nc.sync.dma_start(
                 out=bank_sc[32 * q : 32 * q + 4, :, :].bitcast(I32),
                 in_=bank_scales[:, 4 * q : 4 * q + 4, :].rearrange("g r n -> r g n").bitcast(I32),
             )
         nc.sync.dma_start(out=bank[:], in_=bank_words.rearrange("g p n -> p g n"))
+
+        def spread_scale():
+            for part in range(2):
+                xt = psum.tile([P, 4, P], F32, tag="sum", name="spread", bufs=4)
+                for m in range(4):
+                    col = scale_cols[:, 4 * part + m : 4 * part + m + 1]
+                    nc.tensor.transpose(xt[:, m, :], col.to_broadcast([P, P]), ident[:])
+                empty = nc.scalar.copy if part == 0 else nc.vector.tensor_copy
+                empty(
+                    out=scale_all[:].rearrange("p (n q m) -> p q n m", q=2, m=4)[:, part],
+                    in_=xt[:].rearrange("p m n -> p n m"),
+                )
 
         def cap_turn(t):
             xt = psum.tile([P, PASSES, 2, P], F32, tag="turn", name="xt", bufs=4)
@@ -111,14 +124,23 @@ def tile_siglip_negative_caption_gradient_s13_kernel(
         audio = {}
 
         def widen(g, s):
-            if s == 0:
-                audio[g] = work.tile([P, 4, FEATS], BF16, align_bytes=64, tag="audio", name="audio", bufs=2)
+            audio[g, s] = work.tile([P, FEATS], BF16, align_bytes=64, tag="audio", name="audio", bufs=6)
             nc.vector.tensor_tensor(
-                out=audio[g][:, s, :],
+                out=audio[g, s][:],
                 in0=raw[g][:, s * FEATS : (s + 1) * FEATS].bitcast(FP8),
                 in1=scale_all[:],
                 op=MULT,
             )
+
+        def sort(g, s):
+            if g < SORT:
+                return
+            flat = work.tile([P, FEATS], BF16, align_bytes=64, tag="sorted", name="flat", bufs=4)
+            nc.vector.tensor_copy(
+                out=flat[:].bitcast(F32).rearrange("p (h u w) -> p h u w", h=PASSES, u=2),
+                in_=audio[g, s][:].bitcast(F32).rearrange("p (h w u) -> p h u w", h=PASSES, u=2),
+            )
+            audio[g, s] = flat
 
         def aud_turn(g, top):
             res = []
@@ -126,8 +148,12 @@ def tile_siglip_negative_caption_gradient_s13_kernel(
                 xt = psum.tile([P, 2, 2, P], F32, tag="turn", name="xt", bufs=4)
                 for u in range(2):
                     for e in range(2):
-                        words = audio[g][:, 2 * top + e, :].bitcast(F32)
-                        nc.tensor.transpose(xt[:, u, e, :], words[:, 256 * h + u : 256 * (h + 1) : 2], ident[:])
+                        words = audio[g, 2 * top + e][:].bitcast(F32)
+                        if g < SORT:
+                            words = words[:, 256 * h + u : 256 * (h + 1) : 2]
+                        else:
+                            words = words[:, 256 * h + P * u : 256 * h + P * (u + 1)]
+                        nc.tensor.transpose(xt[:, u, e, :], words, ident[:])
                 grouped = work.tile([P, 1024], BF16, align_bytes=64, tag="grouped", name="aud_grouped", bufs=7)
                 nc.scalar.copy(
                     out=grouped[:].bitcast(F32).rearrange("p (q e u) -> p q e u", e=2, u=2),
@@ -164,7 +190,7 @@ def tile_siglip_negative_caption_gradient_s13_kernel(
             nc.scalar.activation(out=sigs[t, pair][:, g % 2, :], in_=acc[:], func=SIGMOID, bias=bias_cols[:, t : t + 1])
 
         def weigh(t, pair):
-            resids[t, pair] = work.tile([P, 2, CHUNK], BF16, align_bytes=64, tag="resid", name="resid", bufs=12)
+            resids[t, pair] = work.tile([P, 2, CHUNK], BF16, align_bytes=64, tag="resid", name="resid", bufs=10)
             nc.vector.tensor_tensor(
                 out=resids[t, pair][:],
                 in0=sigs[t, pair][:],
@@ -211,17 +237,21 @@ def tile_siglip_negative_caption_gradient_s13_kernel(
 
         def finish(t):
             res = work.tile([P, FEATS], F32, tag="res", name="res")
+            rows = slice(t * P, (t + 1) * P)
             last = t == CAP_TILES - 1
             for h in range(2):
                 cols = slice(512 * h, 512 * (h + 1))
                 if last and h == 1:
-                    nc.vector.tensor_copy(out=res[:, cols], in_=sums[t, h][:])
+                    for x in range(2):
+                        part = slice(512 + 256 * x, 512 + 256 * (x + 1))
+                        nc.vector.tensor_copy(out=res[:, part], in_=sums[t, h][:, 256 * x : 256 * (x + 1)])
+                        nc.sync.dma_start(out=out[rows, part], in_=res[:, part])
                 else:
                     nc.scalar.copy(out=res[:, cols], in_=sums[t, h][:])
-                if last:
-                    nc.sync.dma_start(out=out[t * P : (t + 1) * P, cols], in_=res[:, cols])
+                    if last:
+                        nc.sync.dma_start(out=out[rows, cols], in_=res[:, cols])
             if not last:
-                nc.sync.dma_start(out=out[t * P : (t + 1) * P, :], in_=res[:])
+                nc.sync.dma_start(out=out[rows, :], in_=res[:])
 
         def order_weights():
             for k in range(CHUNKS):
@@ -231,14 +261,14 @@ def tile_siglip_negative_caption_gradient_s13_kernel(
                 )
 
         ctx.enter_context(tc.manual_schedule())
-        widen(0, 0)
+        spread_scale()
         c0 = cap_turn(0)
+        widen(0, 0)
         widen(0, 1)
         c1 = cap_turn(1)
         a0 = aud_turn(0, 0)
         widen(0, 2)
         widen(0, 3)
-        order_weights()
         aud_quant(0, 0, a0)
         bias_ps = psum.tile([P, P], BF16, tag="turn", name="bias_ps", bufs=4)
         nc.tensor.transpose(bias_ps[:], bias_rows[:], ident_b[:])
@@ -268,42 +298,57 @@ def tile_siglip_negative_caption_gradient_s13_kernel(
         cap_quant(4, c4)
         cap_quant(5, c5)
         widen(1, 2)
+        sort(1, 0)
+        sort(1, 1)
         n0 = aud_turn(1, 0)
         c6 = cap_turn(6)
         c7 = cap_turn(7)
         widen(1, 3)
+        sort(1, 2)
         aud_quant(1, 0, n0)
+        sort(1, 3)
         cap_quant(6, c6)
         cap_quant(7, c7)
         widen(2, 0)
         n1 = aud_turn(1, 1)
         for t in range(4, 8):
             logits(t, 0)
+        order_weights()
         aud_quant(1, 1, n1)
         widen(2, 1)
+        sort(2, 0)
         widen(2, 2)
+        sort(2, 1)
         widen(2, 3)
+        sort(2, 2)
         for g in range(1, CHUNKS):
             more = g + 1 < CHUNKS
             for t in range(4):
                 logits(t, g)
+            if g == 1:
+                widen(3, 0)
+                sort(2, 3)
             if more:
                 n0 = aud_turn(g + 1, 0)
                 n1 = aud_turn(g + 1, 1)
             if g == 1:
-                widen(3, 0)
                 widen(3, 1)
+                sort(3, 0)
             if more:
                 aud_quant(g + 1, 0, n0)
             if g == 1:
                 widen(3, 2)
+                sort(3, 1)
             if more:
                 aud_quant(g + 1, 1, n1)
                 for t in range(4, 8):
                     logits(t, g)
             if g == 1:
                 widen(3, 3)
-                for t in range(4):
+                sort(3, 2)
+                weigh(0, 0)
+                sort(3, 3)
+                for t in range(1, 3):
                     weigh(t, 0)
         weigh(0, 1)
         logits(4, 3)
@@ -315,6 +360,7 @@ def tile_siglip_negative_caption_gradient_s13_kernel(
         quants(0, r0)
         logits(6, 3)
         logits(7, 3)
+        weigh(3, 0)
         weigh(3, 1)
         quants(1, r1)
 

@@ -38,7 +38,7 @@ def tile_siglip_negative_caption_gradient_s13_kernel(
         scale_all = keep.tile([P, FEATS], F32, name="scale_all")
         raw = [keep.tile([P, 4 * FEATS], U8, name="raw%d" % g) for g in range(CHUNKS)]
         cap = [keep.tile([P, FEATS], BF16, name="cap%d" % t) for t in range(CAP_TILES)]
-        scale_cols = keep.tile([P, 8], F32, name="scale_cols")
+        scale_cols = keep.tile([P, PASSES, 4], F32, name="scale_cols")
         weight_all = keep.tile([P, CLIPS], BF16, name="weight_all")
         weight_ord = keep.tile([P, CLIPS], BF16, name="weight_ord")
         bias_rows = keep.tile([P, P], BF16, name="bias_rows")
@@ -68,7 +68,7 @@ def tile_siglip_negative_caption_gradient_s13_kernel(
         def load_cap(t):
             nc.sync.dma_start(out=cap[t][:], in_=cap_view[t])
 
-        nc.sync.dma_start(out=scale_cols[:], in_=audio_scale.rearrange("o (n m) -> (o n) m", m=8))
+        nc.sync.dma_start(out=scale_cols[:], in_=audio_scale.rearrange("o (h n m) -> n (o h) m", h=PASSES, m=4))
         nc.sync.dma_start(out=raw[0][:, :half], in_=aud_view[0][:, :half])
         load_cap(0)
         nc.sync.dma_start(out=raw[0][:, half:], in_=aud_view[0][:, half:])
@@ -76,9 +76,9 @@ def tile_siglip_negative_caption_gradient_s13_kernel(
         load_cap(1)
         load_cap(2)
         load_cap(3)
-        nc.sync.dma_start(out=raw[1][:], in_=aud_view[1])
         for t in range(4, CAP_TILES):
             load_cap(t)
+        nc.sync.dma_start(out=raw[1][:], in_=aud_view[1])
         nc.sync.dma_start(out=raw[2][:], in_=aud_view[2])
         nc.sync.dma_start(out=raw[3][:], in_=aud_view[3])
         nc.sync.dma_start(out=weight_all[:], in_=clip_weight.partition_broadcast(P))
@@ -89,17 +89,14 @@ def tile_siglip_negative_caption_gradient_s13_kernel(
             )
         nc.sync.dma_start(out=bank[:], in_=bank_words.rearrange("g p n -> p g n"))
 
-        def spread_scale():
-            for part in range(2):
-                xt = psum.tile([P, 4, P], F32, tag="sum", name="spread", bufs=4)
-                for m in range(4):
-                    col = scale_cols[:, 4 * part + m : 4 * part + m + 1]
-                    nc.tensor.transpose(xt[:, m, :], col.to_broadcast([P, P]), ident[:])
-                empty = nc.scalar.copy if part == 0 else nc.vector.tensor_copy
-                empty(
-                    out=scale_all[:].rearrange("p (n q m) -> p q n m", q=2, m=4)[:, part],
-                    in_=xt[:].rearrange("p m n -> p n m"),
-                )
+        def spread_scale(h):
+            xt = psum.tile([P, 4, P], F32, tag="sum", name="spread", bufs=4)
+            for m in range(4):
+                nc.tensor.transpose(xt[:, m, :], scale_cols[:, h, m : m + 1].to_broadcast([P, P]), ident[:])
+            nc.scalar.copy(
+                out=scale_all[:, CHUNK * h : CHUNK * (h + 1)].rearrange("p (n m) -> p n m", m=4),
+                in_=xt[:].rearrange("p m n -> p n m"),
+            )
 
         def cap_turn(t):
             xt = psum.tile([P, PASSES, 2, P], F32, tag="turn", name="xt", bufs=4)
@@ -123,12 +120,13 @@ def tile_siglip_negative_caption_gradient_s13_kernel(
 
         audio = {}
 
-        def widen(g, s):
-            audio[g, s] = work.tile([P, FEATS], BF16, align_bytes=64, tag="audio", name="audio", bufs=6)
+        def widen(g, s, first=0, end=FEATS):
+            if first == 0:
+                audio[g, s] = work.tile([P, FEATS], BF16, align_bytes=64, tag="audio", name="audio", bufs=6)
             nc.vector.tensor_tensor(
-                out=audio[g, s][:],
-                in0=raw[g][:, s * FEATS : (s + 1) * FEATS].bitcast(FP8),
-                in1=scale_all[:],
+                out=audio[g, s][:, first:end],
+                in0=raw[g][:, s * FEATS + first : s * FEATS + end].bitcast(FP8),
+                in1=scale_all[:, first:end],
                 op=MULT,
             )
 
@@ -142,9 +140,9 @@ def tile_siglip_negative_caption_gradient_s13_kernel(
             )
             audio[g, s] = flat
 
-        def aud_turn(g, top):
+        def aud_turn(g, top, halves=range(PASSES)):
             res = []
-            for h in range(PASSES):
+            for h in halves:
                 xt = psum.tile([P, 2, 2, P], F32, tag="turn", name="xt", bufs=4)
                 for u in range(2):
                     for e in range(2):
@@ -254,37 +252,40 @@ def tile_siglip_negative_caption_gradient_s13_kernel(
                 nc.sync.dma_start(out=out[rows, :], in_=res[:])
 
         def order_weights():
-            for k in range(CHUNKS):
-                nc.scalar.copy(
-                    out=weight_ord[:].rearrange("p (g u q e) -> p g u q e", g=CHUNKS, u=2, e=2)[:, k],
-                    in_=weight_all[:].rearrange("p (g q u e) -> p g u q e", g=CHUNKS, u=2, e=2)[:, k],
-                )
+            nc.vector.tensor_copy(
+                out=weight_ord[:].bitcast(F32).rearrange("p (g u q) -> p g u q", g=CHUNKS, u=2),
+                in_=weight_all[:].bitcast(F32).rearrange("p (g q u) -> p g u q", g=CHUNKS, u=2),
+            )
 
         ctx.enter_context(tc.manual_schedule())
-        spread_scale()
+        for h in range(PASSES):
+            spread_scale(h)
         c0 = cap_turn(0)
-        widen(0, 0)
-        widen(0, 1)
+        for h in range(PASSES):
+            for s in range(2):
+                widen(0, s, CHUNK * h, CHUNK * (h + 1))
+        a0 = aud_turn(0, 0, [0])
         c1 = cap_turn(1)
-        a0 = aud_turn(0, 0)
-        widen(0, 2)
-        widen(0, 3)
-        aud_quant(0, 0, a0)
+        a0 += aud_turn(0, 0, [1])
         bias_ps = psum.tile([P, P], BF16, tag="turn", name="bias_ps", bufs=4)
         nc.tensor.transpose(bias_ps[:], bias_rows[:], ident_b[:])
+        widen(0, 2)
+        c2 = cap_turn(2)
+        widen(0, 3)
+        c3 = cap_turn(3)
+        aud_quant(0, 0, a0)
         cap_quant(0, c0)
         cap_quant(1, c1)
-        nc.vector.tensor_copy(out=bias_cols[:], in_=bias_ps[:, 0:CAP_TILES])
         a1 = aud_turn(0, 1)
-        c2 = cap_turn(2)
-        aud_quant(0, 1, a1)
-        c3 = cap_turn(3)
-        cap_quant(2, c2)
-        widen(1, 0)
-        cap_quant(3, c3)
-        widen(1, 1)
         c4 = cap_turn(4)
+        cap_quant(2, c2)
+        nc.vector.tensor_copy(out=bias_cols[:], in_=bias_ps[:, 0:CAP_TILES])
+        aud_quant(0, 1, a1)
+        cap_quant(3, c3)
+        widen(1, 0)
         c5 = cap_turn(5)
+        cap_quant(4, c4)
+        widen(1, 1)
 
         def turns(t):
             return [pair_turn(t, 0), pair_turn(t, 1)]
@@ -293,27 +294,23 @@ def tile_siglip_negative_caption_gradient_s13_kernel(
             pair_quant(t, 0, r[0])
             pair_quant(t, 1, r[1])
 
-        for t in range(4):
+        for t in range(3):
             logits(t, 0)
-        cap_quant(4, c4)
-        cap_quant(5, c5)
         widen(1, 2)
-        sort(1, 0)
-        sort(1, 1)
-        n0 = aud_turn(1, 0)
         c6 = cap_turn(6)
-        c7 = cap_turn(7)
+        n0 = aud_turn(1, 0)
+        cap_quant(5, c5)
         widen(1, 3)
-        sort(1, 2)
-        aud_quant(1, 0, n0)
-        sort(1, 3)
-        cap_quant(6, c6)
-        cap_quant(7, c7)
-        widen(2, 0)
-        n1 = aud_turn(1, 1)
-        for t in range(4, 8):
+        for t in range(3, 5):
             logits(t, 0)
-        order_weights()
+        aud_quant(1, 0, n0)
+        cap_quant(6, c6)
+        c7 = cap_turn(7)
+        n1 = aud_turn(1, 1)
+        widen(2, 0)
+        cap_quant(7, c7)
+        for t in range(5, 8):
+            logits(t, 0)
         aud_quant(1, 1, n1)
         widen(2, 1)
         sort(2, 0)
@@ -337,19 +334,20 @@ def tile_siglip_negative_caption_gradient_s13_kernel(
             if more:
                 aud_quant(g + 1, 0, n0)
             if g == 1:
-                widen(3, 2)
                 sort(3, 1)
             if more:
                 aud_quant(g + 1, 1, n1)
                 for t in range(4, 8):
                     logits(t, g)
             if g == 1:
+                widen(3, 2)
                 widen(3, 3)
                 sort(3, 2)
-                weigh(0, 0)
                 sort(3, 3)
-                for t in range(1, 3):
-                    weigh(t, 0)
+                order_weights()
+                weigh(0, 0)
+                weigh(1, 0)
+        weigh(2, 0)
         weigh(0, 1)
         logits(4, 3)
         weigh(1, 1)
@@ -380,16 +378,16 @@ def tile_siglip_negative_caption_gradient_s13_kernel(
         finish(2)
         r4 = turns(4)
         r5 = turns(5)
-        quants(4, r4)
         weigh(6, 0)
+        quants(4, r4)
         weigh(6, 1)
         quants(5, r5)
+        weigh(7, 0)
+        weigh(7, 1)
         grad(3)
         finish(3)
         grad(4)
         finish(4)
-        weigh(7, 0)
-        weigh(7, 1)
         r6 = turns(6)
         r7 = turns(7)
         quants(6, r6)

from contextlib import ExitStack

import concourse.mybir as mybir
from concourse.masks import make_identity

F32 = mybir.dt.float32
BF16 = mybir.dt.bfloat16
U32 = mybir.dt.uint32
I32 = mybir.dt.int32
U8 = mybir.dt.uint8
FP8 = mybir.dt.float8_e4m3fn
FP8X4 = mybir.dt.float8_e4m3fn_x4
FP4X4 = mybir.dt.float4_e2m1fn_x4
MULT = mybir.AluOpType.mult
SIGMOID = mybir.ActivationFunctionType.Sigmoid

CLIPS, CAPS, FEATS = 2048, 1024, 1024
P = 128
CHUNK = 512
CHUNKS = CLIPS // CHUNK
PASSES = FEATS // CHUNK
CAP_TILES = CAPS // P

SORT = 3

FLOPS = 2 * 2 * CLIPS * CAPS * FEATS


def tile_siglip_negative_caption_gradient_s13_kernel(
    tc, audio_bytes, audio_scale, captions, bias, clip_weight, bank_words, bank_scales, out
):
    nc = tc.nc
    with ExitStack() as ctx:
        keep = ctx.enter_context(tc.tile_pool(name="keep", bufs=1))
        work = ctx.enter_context(tc.tile_pool(name="work", bufs=3))
        psum = ctx.enter_context(tc.psum_pool(name="psum", bufs=2))

        scale_all = keep.tile([P, FEATS], F32, name="scale_all")
        raw = [keep.tile([P, 4 * FEATS], U8, name="raw%d" % g) for g in range(CHUNKS)]
        cap = [keep.tile([P, FEATS], BF16, name="cap%d" % t) for t in range(CAP_TILES)]
        scale_cols = keep.tile([P, PASSES, 4], F32, name="scale_cols")
        weight_all = keep.tile([P, CLIPS], BF16, name="weight_all")
        weight_ord = keep.tile([P, CLIPS], BF16, name="weight_ord")
        bias_rows = keep.tile([P, P], BF16, name="bias_rows")
        bias_cols = keep.tile([P, CAP_TILES], F32, name="bias_cols")
        bank = keep.tile([P, CHUNKS, 2 * FEATS], U8, align_bytes=64, name="bank")
        bank_sc = keep.tile([P, CHUNKS, FEATS], U8, align_bytes=64, name="bank_sc")
        ident = keep.tile([P, P], F32, name="ident")
        ident_b = keep.tile([P, P], BF16, name="ident_b")
        dummy = keep.tile([P, 1], F32, name="dummy")
        aud_codes = keep.tile([P, CHUNKS, PASSES, CHUNK], U32, align_bytes=64, name="aud_codes")
        aud_planes = keep.tile([P, CHUNKS, PASSES, CHUNK], U8, align_bytes=64, name="aud_planes")
        cap_codes = keep.tile([P, CAP_TILES, PASSES, P], U32, align_bytes=64, name="cap_codes")
        cap_planes = keep.tile([P, CAP_TILES, PASSES, P], U8, align_bytes=64, name="cap_planes")
        r_codes = keep.tile([P, CAP_TILES, CHUNKS, P], U32, align_bytes=64, name="r_codes")
        r_planes = keep.tile([P, CAP_TILES, CHUNKS, P], U8, align_bytes=64, name="r_planes")

        nc.vector.memset(dummy[:], 0.0)
        nc.vector.memset(bias_rows[:], 0.0)
        nc.scalar.activation(out=dummy[:], in_=dummy[:], func=SIGMOID)
        make_identity(nc, ident[:])
        make_identity(nc, ident_b[:])
        nc.gpsimd.memset(bank_sc[:].rearrange("p g d -> p (g d)").bitcast(U32), 0)

        aud_view = audio_bytes.rearrange("(g q s) d -> g q (s d)", q=P, s=4)
        cap_view = captions.rearrange("(t p) d -> t p d", p=P)
        half = 2 * FEATS
        def load_cap(t):
            nc.sync.dma_start(out=cap[t][:], in_=cap_view[t])

        nc.sync.dma_start(out=scale_cols[:], in_=audio_scale.rearrange("o (h n m) -> n (o h) m", h=PASSES, m=4))
        nc.sync.dma_start(out=raw[0][:, :half], in_=aud_view[0][:, :half])
        load_cap(0)
        nc.sync.dma_start(out=raw[0][:, half:], in_=aud_view[0][:, half:])
        nc.sync.dma_start(out=bias_rows[0:CAP_TILES, :], in_=bias.rearrange("(t p) -> t p", p=P))
        load_cap(1)
        load_cap(2)
        load_cap(3)
        for t in range(4, CAP_TILES):
            load_cap(t)
        nc.sync.dma_start(out=raw[1][:], in_=aud_view[1])
        nc.sync.dma_start(out=raw[2][:], in_=aud_view[2])
        nc.sync.dma_start(out=raw[3][:], in_=aud_view[3])
        nc.sync.dma_start(out=weight_all[:], in_=clip_weight.partition_broadcast(P))
        for q in range(4):
            nc.sync.dma_start(
                out=bank_sc[32 * q : 32 * q + 4, :, :].bitcast(I32),
                in_=bank_scales[:, 4 * q : 4 * q + 4, :].rearrange("g r n -> r g n").bitcast(I32),
            )
        nc.sync.dma_start(out=bank[:], in_=bank_words.rearrange("g p n -> p g n"))

        def spread_scale(h):
            xt = psum.tile([P, 4, P], F32, tag="sum", name="spread", bufs=4)
            for m in range(4):
                nc.tensor.transpose(xt[:, m, :], scale_cols[:, h, m : m + 1].to_broadcast([P, P]), ident[:])
            nc.scalar.copy(
                out=scale_all[:, CHUNK * h : CHUNK * (h + 1)].rearrange("p (n m) -> p n m", m=4),
                in_=xt[:].rearrange("p m n -> p n m"),
            )

        def cap_turn(t):
            xt = psum.tile([P, PASSES, 2, P], F32, tag="turn", name="xt", bufs=4)
            words = cap[t][:].bitcast(F32)
            for h in range(PASSES):
                for u in range(2):
                    nc.tensor.transpose(xt[:, h, u, :], words[:, 256 * h + u : 256 * (h + 1) : 2], ident[:])
            grouped = work.tile([P, 1024], BF16, align_bytes=64, tag="grouped", name="cap_grouped", bufs=7)
            nc.scalar.copy(
                out=grouped[:].bitcast(F32).rearrange("p (h j u) -> p h j u", h=PASSES, u=2),
                in_=xt[:].rearrange("p h u j -> p h j u"),
            )
            return grouped

        def cap_quant(t, grouped):
            nc.vector.quantize_mx(
                out=cap_codes[:, t, :, :].rearrange("p h j -> p (h j)").bitcast(FP8X4),
                scales=cap_planes[:, t, :, :].rearrange("p h j -> p (h j)"),
                in_=grouped[:],
            )

        audio = {}

        def widen(g, s, first=0, end=FEATS):
            if first == 0:
                audio[g, s] = work.tile([P, FEATS], BF16, align_bytes=64, tag="audio", name="audio", bufs=6)
            nc.vector.tensor_tensor(
                out=audio[g, s][:, first:end],
                in0=raw[g][:, s * FEATS + first : s * FEATS + end].bitcast(FP8),
                in1=scale_all[:, first:end],
                op=MULT,
            )

        def sort(g, s):
            if g < SORT:
                return
            flat = work.tile([P, FEATS], BF16, align_bytes=64, tag="sorted", name="flat", bufs=4)
            nc.vector.tensor_copy(
                out=flat[:].bitcast(F32).rearrange("p (h u w) -> p h u w", h=PASSES, u=2),
                in_=audio[g, s][:].bitcast(F32).rearrange("p (h w u) -> p h u w", h=PASSES, u=2),
            )
            audio[g, s] = flat

        def aud_turn(g, top, halves=range(PASSES)):
            res = []
            for h in halves:
                xt = psum.tile([P, 2, 2, P], F32, tag="turn", name="xt", bufs=4)
                for u in range(2):
                    for e in range(2):
                        words = audio[g, 2 * top + e][:].bitcast(F32)
                        if g < SORT:
                            words = words[:, 256 * h + u : 256 * (h + 1) : 2]
                        else:
                            words = words[:, 256 * h + P * u : 256 * h + P * (u + 1)]
                        nc.tensor.transpose(xt[:, u, e, :], words, ident[:])
                grouped = work.tile([P, 1024], BF16, align_bytes=64, tag="grouped", name="aud_grouped", bufs=7)
                nc.scalar.copy(
                    out=grouped[:].bitcast(F32).rearrange("p (q e u) -> p q e u", e=2, u=2),
                    in_=xt[:].rearrange("p u e q -> p q e u"),
                )
                res.append(grouped)
            return res

        def aud_quant(g, top, res):
            for h in range(PASSES):
                cols = slice(256 * top, 256 * (top + 1))
                nc.vector.quantize_mx(
                    out=aud_codes[:, g, h, cols].bitcast(FP8X4), scales=aud_planes[:, g, h, cols], in_=res[h][:]
                )

        sigs = {}
        resids = {}

        def logits(t, g):
            pair = g // 2
            if g % 2 == 0:
                sigs[t, pair] = work.tile([P, 2, CHUNK], F32, tag="sig", name="sig", bufs=16)
            acc = psum.tile([P, CHUNK], F32, tag="sum", name="acc", bufs=4)
            for h in range(PASSES):
                nc.tensor.matmul_mx(
                    out=acc[:],
                    lhsT=cap_codes[:, t, h, :].bitcast(FP8X4),
                    lhsT_scale=cap_planes[:, t, h, :],
                    rhs=aud_codes[:, g, h, :].bitcast(FP8X4),
                    rhs_scale=aud_planes[:, g, h, :],
                    start=(h == 0),
                    stop=(h == PASSES - 1),
                )
            nc.scalar.activation(out=sigs[t, pair][:, g % 2, :], in_=acc[:], func=SIGMOID, bias=bias_cols[:, t : t + 1])

        def weigh(t, pair):
            resids[t, pair] = work.tile([P, 2, CHUNK], BF16, align_bytes=64, tag="resid", name="resid", bufs=10)
            nc.vector.tensor_tensor(
                out=resids[t, pair][:],
                in0=sigs[t, pair][:],
                in1=weight_ord[:, 2 * CHUNK * pair : 2 * CHUNK * (pair + 1)].rearrange("p (a c) -> p a c", a=2),
                op=MULT,
            )

        def pair_turn(t, pair):
            xt = psum.tile([P, 2, 2, P], F32, tag="turn", name="xt", bufs=4)
            for a in range(2):
                words = resids[t, pair][:, a, :].bitcast(F32)
                for top in range(2):
                    nc.tensor.transpose(xt[:, a, top, :], words[:, P * top : P * (top + 1)], ident[:])
            grouped = work.tile([P, 1024], BF16, align_bytes=64, tag="grouped", name="r_grouped", bufs=7)
            nc.scalar.copy(
                out=grouped[:].bitcast(F32).rearrange("p (a j u) -> p a j u", a=2, u=2),
                in_=xt[:].rearrange("p a u j -> p a j u"),
            )
            return grouped

        def pair_quant(t, pair, grouped):
            two = slice(2 * pair, 2 * pair + 2)
            nc.vector.quantize_mx(
                out=r_codes[:, t, two, :].rearrange("p a j -> p (a j)").bitcast(FP8X4),
                scales=r_planes[:, t, two, :].rearrange("p a j -> p (a j)"),
                in_=grouped[:],
            )

        sums = {}

        def grad(t):
            for h in range(2):
                sums[t, h] = psum.tile([P, 512], F32, tag="sum", name="gradsum", bufs=4)
                for g in range(CHUNKS):
                    nc.tensor.matmul_mx(
                        out=sums[t, h][:],
                        lhsT=r_codes[:, t, g, :].bitcast(FP8X4),
                        lhsT_scale=r_planes[:, t, g, :],
                        rhs=bank[:, g, 1024 * h : 1024 * (h + 1)].bitcast(FP4X4),
                        rhs_scale=bank_sc[:, g, 512 * h : 512 * (h + 1)],
                        start=(g == 0),
                        stop=(g == CHUNKS - 1),
                    )

        def finish(t):
            res = work.tile([P, FEATS], F32, tag="res", name="res")
            rows = slice(t * P, (t + 1) * P)
            last = t == CAP_TILES - 1
            for h in range(2):
                cols = slice(512 * h, 512 * (h + 1))
                if last and h == 1:
                    for x in range(2):
                        part = slice(512 + 256 * x, 512 + 256 * (x + 1))
                        nc.vector.tensor_copy(out=res[:, part], in_=sums[t, h][:, 256 * x : 256 * (x + 1)])
                        nc.sync.dma_start(out=out[rows, part], in_=res[:, part])
                else:
                    nc.scalar.copy(out=res[:, cols], in_=sums[t, h][:])
                    if last:
                        nc.sync.dma_start(out=out[rows, cols], in_=res[:, cols])
            if not last:
                nc.sync.dma_start(out=out[rows, :], in_=res[:])

        def order_weights():
            nc.vector.tensor_copy(
                out=weight_ord[:].bitcast(F32).rearrange("p (g u q) -> p g u q", g=CHUNKS, u=2),
                in_=weight_all[:].bitcast(F32).rearrange("p (g q u) -> p g u q", g=CHUNKS, u=2),
            )

        ctx.enter_context(tc.manual_schedule())
        for h in range(PASSES):
            spread_scale(h)
        c0 = cap_turn(0)
        for h in range(PASSES):
            for s in range(2):
                widen(0, s, CHUNK * h, CHUNK * (h + 1))
        a0 = aud_turn(0, 0, [0])
        c1 = cap_turn(1)
        a0 += aud_turn(0, 0, [1])
        bias_ps = psum.tile([P, P], BF16, tag="turn", name="bias_ps", bufs=4)
        nc.tensor.transpose(bias_ps[:], bias_rows[:], ident_b[:])
        widen(0, 2)
        c2 = cap_turn(2)
        widen(0, 3)
        c3 = cap_turn(3)
        aud_quant(0, 0, a0)
        cap_quant(0, c0)
        cap_quant(1, c1)
        a1 = aud_turn(0, 1)
        c4 = cap_turn(4)
        cap_quant(2, c2)
        nc.vector.tensor_copy(out=bias_cols[:], in_=bias_ps[:, 0:CAP_TILES])
        aud_quant(0, 1, a1)
        cap_quant(3, c3)
        widen(1, 0)
        c5 = cap_turn(5)
        cap_quant(4, c4)
        widen(1, 1)

        def turns(t):
            return [pair_turn(t, 0), pair_turn(t, 1)]

        def quants(t, r):
            pair_quant(t, 0, r[0])
            pair_quant(t, 1, r[1])

        for t in range(3):
            logits(t, 0)
        widen(1, 2)
        c6 = cap_turn(6)
        n0 = aud_turn(1, 0)
        cap_quant(5, c5)
        widen(1, 3)
        for t in range(3, 5):
            logits(t, 0)
        aud_quant(1, 0, n0)
        cap_quant(6, c6)
        c7 = cap_turn(7)
        n1 = aud_turn(1, 1)
        widen(2, 0)
        cap_quant(7, c7)
        for t in range(5, 8):
            logits(t, 0)
        aud_quant(1, 1, n1)
        widen(2, 1)
        sort(2, 0)
        widen(2, 2)
        sort(2, 1)
        widen(2, 3)
        sort(2, 2)
        for g in range(1, CHUNKS):
            more = g + 1 < CHUNKS
            for t in range(4):
                logits(t, g)
            if g == 1:
                widen(3, 0)
                sort(2, 3)
            if more:
                n0 = aud_turn(g + 1, 0)
                n1 = aud_turn(g + 1, 1)
            if g == 1:
                widen(3, 1)
                sort(3, 0)
            if more:
                aud_quant(g + 1, 0, n0)
            if g == 1:
                sort(3, 1)
            if more:
                aud_quant(g + 1, 1, n1)
                for t in range(4, 8):
                    logits(t, g)
            if g == 1:
                widen(3, 2)
                widen(3, 3)
                sort(3, 2)
                sort(3, 3)
                order_weights()
                weigh(0, 0)
                weigh(1, 0)
        weigh(2, 0)
        weigh(0, 1)
        logits(4, 3)
        weigh(1, 1)
        logits(5, 3)
        weigh(2, 1)
        r0 = turns(0)
        r1 = turns(1)
        quants(0, r0)
        logits(6, 3)
        logits(7, 3)
        weigh(3, 0)
        weigh(3, 1)
        quants(1, r1)

        grad(0)
        finish(0)
        r2 = turns(2)
        r3 = turns(3)
        weigh(4, 0)
        quants(2, r2)
        weigh(4, 1)
        quants(3, r3)
        grad(1)
        finish(1)
        weigh(5, 0)
        weigh(5, 1)
        grad(2)
        finish(2)
        r4 = turns(4)
        r5 = turns(5)
        weigh(6, 0)
        quants(4, r4)
        weigh(6, 1)
        quants(5, r5)
        weigh(7, 0)
        weigh(7, 1)
        grad(3)
        finish(3)
        grad(4)
        finish(4)
        r6 = turns(6)
        r7 = turns(7)
        quants(6, r6)
        quants(7, r7)
        grad(5)
        finish(5)
        grad(6)
        finish(6)
        grad(7)
        finish(7)
